import numpy as np
import ml_dtypes


def mxq(x, axis, fmt="e4m3"):
    dtype, down = {"e4m3": (ml_dtypes.float8_e4m3fn, 7), "e5m2": (ml_dtypes.float8_e5m2, 14)}[fmt]
    v = np.moveaxis(np.asarray(x, np.float32).astype(ml_dtypes.bfloat16).astype(np.float64), axis, -1)
    blocks = v.reshape(v.shape[:-1] + (-1, 32))
    amax = np.abs(blocks).max(-1, keepdims=True)
    byte = np.maximum(np.where(amax > 0, np.frexp(amax)[1] - 1 + 127, 0) - down, 1)
    scale = np.exp2(byte - 127.0)
    codes = (blocks / scale).astype(np.float32).astype(dtype).astype(np.float64)
    return np.moveaxis((codes * scale).reshape(v.shape), -1, axis)


WIDE = False


def mx_kscale(k):
    if not WIDE:
        return np.ones(k)
    levels = np.array([10, -10, 5, -5, 0])
    if k % 512:
        return np.exp2(np.random.permutation(np.resize(levels, k // 32))).repeat(32)
    a = np.empty((k // 512, 16))
    for p in range(k // 512):
        a[p, :8] = np.random.permutation(np.resize(levels, 8))
        for g in range(8):
            far = levels[np.abs(levels - a[p, g]) >= 10]
            a[p, g + 8] = far[np.random.randint(len(far))]
    return np.exp2(a.ravel()).repeat(32)


def f64(x):
    return np.asarray(x).astype(np.float64)


def striped(idx):
    return np.tile(np.asarray(idx).reshape(-1, 16).T, (8, 1)).astype(np.uint16)


def unstriped(offs):
    return offs[:16].T.reshape(-1).astype(np.int64)


def striped8(idx):
    return np.asarray(idx).reshape(8, -1, 16).transpose(0, 2, 1).reshape(128, -1).astype(np.uint16)


def unstriped8(offs):
    return offs.reshape(8, 16, -1).transpose(0, 2, 1).reshape(8, -1).astype(np.int64)


def pick8(x, idx, run):
    r = np.arange(len(x))
    return x[r[:, None], idx[r % (8 * run) // run]]


E2M1 = np.array([0.0, 0.5, 1.0, 1.5, 2.0, 3.0, 4.0, 6.0, -0.0, -0.5, -1.0, -1.5, -2.0, -3.0, -4.0, -6.0])


def pack_weight(w, fmt):
    k, n = w.shape
    w = f64(np.asarray(w, np.float32).astype(ml_dtypes.bfloat16)).reshape(k // 32, 32, n)
    amax = np.abs(w).max(1)
    if fmt == "e4m3":
        byte = np.frexp(amax)[1] - 1 + 127 - 7
    else:
        mant, ex = np.frexp(amax / 6.0)
        byte = np.where(mant > 0.5, ex, ex - 1) + 127
    byte = np.clip(np.where(amax > 0, byte, 1), 1, 254)
    scaled = (w * np.exp2(127.0 - byte)[:, None, :]).reshape(k, n).astype(np.float32)
    by_word = np.ascontiguousarray(scaled.reshape(k // 512, 128, 4, n).transpose(0, 1, 3, 2))
    if fmt == "e4m3":
        words = by_word.astype(ml_dtypes.float8_e4m3fn).view(np.uint8)
    else:
        c = by_word.astype(ml_dtypes.float4_e2m1fn).view(np.uint8) & 0xF
        words = (c[..., 0::2] | (c[..., 1::2] << 4)).reshape(k // 512, 128, 2 * n)
    return np.ascontiguousarray(words), np.ascontiguousarray(byte.astype(np.uint8).reshape(k // 512, 16, n))


def unpack_weight(words, scales, fmt):
    g, _, n = scales.shape
    words = np.ascontiguousarray(words).reshape(g, 128, n, -1)
    if fmt == "e4m3":
        vals = words.view(ml_dtypes.float8_e4m3fn).astype(np.float64)
    else:
        nib = np.empty((g, 128, n, 4), np.uint8)
        nib[..., 0::2] = words & 0xF
        nib[..., 1::2] = words >> 4
        vals = E2M1[nib]
    vals = vals * np.repeat(np.exp2(scales.astype(np.float64) - 127.0), 8, axis=1)[..., None]
    return vals.transpose(0, 1, 3, 2).reshape(g * 512, n)


def sigmoid(v):
    return 1.0 / (1.0 + np.exp(-v))


K, R, F, T, J, M = 512, 128, 512, 2048, 512, 256


def setup_inputs():
    n = np.random.standard_normal
    idx = np.random.permutation(T)[:J]
    idx2 = np.stack([np.random.permutation(J)[:M] for _ in range(8)])
    fk = mx_kscale(K)
    ff = mx_kscale(F)
    tabp = pack_weight(n((K, T)) / fk[:, None], "e4m3")
    dtabp = pack_weight(n((K, T)) / fk[:, None], "e4m3")
    return {
        "tab_words": tabp[0],
        "tab_scales": tabp[1],
        "w1": (n((K, R)) * 1 / np.sqrt(K) * fk[:, None]).astype(np.float32),
        "bias": (np.random.uniform(-0.5, 0.5, (R, 1))).astype(np.float32),
        "gain": (np.random.uniform(0.5, 1.5, (R, 1))).astype(np.float32),
        "pw": (np.random.uniform(0.5, 1.5, (1, M))).astype(np.float32),
        "wo": (n((F, R)) * 1 / np.sqrt(F) * ff[:, None]).astype(np.float32),
        "dy": (n((F, M)) / ff[:, None]).astype(np.float32),
        "dtab_words": dtabp[0],
        "dtab_scales": dtabp[1],
        "og": (np.random.uniform(0.7, 2.0, (R, 1))).astype(np.float32),
        "base": (0.3 * n((R, J))).astype(np.float32),
        "offs": striped(idx),
        "offs2": striped8(idx2),
    }


def reference(tab_words, tab_scales, w1, bias, gain, pw, wo, dy, dtab_words, dtab_scales, og, base, offs, offs2):
    idx = unstriped(offs)
    idx2 = unstriped8(offs2)
    tabu = unpack_weight(tab_words, tab_scales, "e4m3")
    dtabu = unpack_weight(dtab_words, dtab_scales, "e4m3")
    w1q = mxq(f64(w1), 0, "e4m3")
    tabidxg = tabu[:, idx]
    a = w1q.T @ tabidxg
    dtabidxg = dtabu[:, idx]
    ta = w1q.T @ dtabidxg
    h1 = np.tanh(a + f64(bias))
    h2 = h1 * f64(gain)
    s = pick8(h2, idx2, 16) * f64(pw)
    woq = mxq(f64(wo), 0, "e4m3")
    dyq = mxq(f64(dy), 0, "e4m3")
    c0 = woq.T @ dyq
    ds = c0 * sigmoid(s) * (1.0 + s * (1.0 - sigmoid(s)))
    e1 = ds * f64(pw)
    s1 = np.zeros((R, J))
    s1[np.arange(R)[:, None], idx2[np.arange(R) % 128 // 16]] = e1
    dh1 = s1 * f64(gain)
    xh1 = ta * (1.0 - np.square(h1))
    xh2 = xh1 * f64(gain)
    xs = pick8(xh2, idx2, 16) * f64(pw)
    xds = (xs * sigmoid(s) * (1.0 - sigmoid(s)) * (1.0 + s * (1.0 - sigmoid(s))) + (xs * (1.0 - sigmoid(s)) + xs * sigmoid(s) * (1.0 - sigmoid(s)) * (-1.0) * s) * sigmoid(s)) * c0
    xe1 = xds * f64(pw)
    xs1 = np.zeros((R, J))
    xs1[np.arange(R)[:, None], idx2[np.arange(R) % 128 // 16]] = xe1
    xdh1 = xs1 * f64(gain)
    xda = xdh1 * (1.0 - np.square(h1)) + xh1 * h1 * 2.0 * (-1.0) * dh1
    y = xda * f64(og) + f64(base)
    return y

@@ -1,0 +1,221 @@
+from contextlib import ExitStack
+
+import concourse.mybir as mybir
+from concourse.masks import make_identity
+
+K, R, F, T, J, M = 512, 128, 512, 2048, 512, 256
+FLOPS = 2 * K * R * J * 2 + 2 * F * R * M
+
+F32 = mybir.dt.float32
+BF16 = mybir.dt.bfloat16
+I32 = mybir.dt.int32
+U32 = mybir.dt.uint32
+U16 = mybir.dt.uint16
+U8 = mybir.dt.uint8
+FP8X4 = mybir.dt.float8_e4m3fn_x4
+ALU = mybir.AluOpType
+ACT = mybir.ActivationFunctionType
+
+P = 128
+PACK = 4
+HALF = J // 2
+LIST_ROWS = 16
+TINY = 2.0**-126
+
+
+def tile_attend_hvpickact_kernel(
+    tc, tab_words, tab_scales, w1, bias, gain, pw, wo, dy, dtab_words, dtab_scales, og, base, offs, offs2, out
+):
+    nc = tc.nc
+    with ExitStack() as ctx:
+        sb = ctx.enter_context(tc.tile_pool(name="sb", bufs=1))
+        ps = ctx.enter_context(tc.psum_pool(name="ps", bufs=1))
+
+        def new(name, width, dtype=F32, tag=None):
+            return sb.tile([P, width], dtype, name=name, tag=tag or name, align_bytes=64)
+
+        slot_list = sb.tile([P, J // LIST_ROWS], U16, name="slot_list")
+        nc.sync.dma_start(slot_list[:], offs)
+
+        def load_scales(name, scales):
+            window = new(name, T, U8)
+            nc.vector.memset(window[:].bitcast(I32), 0)
+            for q in range(4):
+                nc.sync.dma_start(
+                    out=window[32 * q : 32 * q + 4, :].bitcast(I32), in_=scales[0, 4 * q : 4 * q + 4, :].bitcast(I32)
+                )
+            return window
+
+        def load_words(name, words):
+            window = new(name, T, U32)
+            nc.sync.dma_start(out=window[:].bitcast(I32), in_=words[0].rearrange("p n t -> p (n t)").bitcast(I32))
+            return window
+
+        def load_rows(name, rows):
+            raw = sb.tile([P, PACK, rows.shape[1]], F32, name=name)
+            nc.sync.dma_start(out=raw[:], in_=rows.rearrange("(p t) c -> p t c", t=PACK))
+            return raw
+
+        def load_column(name, column):
+            tile = new(name, 1)
+            nc.gpsimd.dma_start(out=tile[:], in_=column)
+            return tile
+
+        w1_raw = load_rows("w1_raw", w1)
+        pick_list = sb.tile([P, M // LIST_ROWS], U16, name="pick_list")
+        nc.sync.dma_start(pick_list[:], offs2)
+        tab_scale_win = load_scales("tab_scale_win", tab_scales)
+        warm = new("warm", 1)
+        warm_out = new("warm_out", 1)
+        nc.gpsimd.memset(warm[:], 0.0)
+        nc.scalar.activation(out=warm_out[:], in_=warm[:], func=ACT.Silu)
+        tab_word_win = load_words("tab_word_win", tab_words)
+        dtab_scale_win = load_scales("dtab_scale_win", dtab_scales)
+        wo_raw = load_rows("wo_raw", wo)
+        dy_raw = load_rows("dy_raw", dy)
+        dtab_word_win = load_words("dtab_word_win", dtab_words)
+        base_sb = new("base_sb", J)
+        nc.sync.dma_start(out=base_sb[:], in_=base)
+
+        b = load_column("b", bias)
+        g = load_column("g", gain)
+        pw_cols = new("pw_cols", M // P)
+        with nc.allow_non_contiguous_dma(reason="one pick weight to a partition"):
+            nc.gpsimd.dma_start(out=pw_cols[:], in_=pw.rearrange("o (t p) -> p (o t)", p=P))
+        o = load_column("o", og)
+
+        placed = new("placed", J)
+        nc.vector.memset(placed[:], 0.0)
+        ident = new("ident", P)
+        make_identity(nc, ident[:])
+
+        def interleave(name, raw, copy):
+            width = raw.shape[2]
+            grouped = new(name, width * PACK, BF16)
+            copy(
+                out=grouped[:].rearrange("p (c i t) -> p c t i", i=4, t=PACK),
+                in_=raw[:].rearrange("p t (c i) -> p c t i", i=4),
+            )
+            return grouped
+
+        def quantize(name, grouped):
+            width = grouped.shape[1] // PACK
+            codes = new(name + "_codes", width, U32)
+            scales = new(name + "_scales", width, U8)
+            nc.vector.quantize_mx(out=codes[:].bitcast(FP8X4), scales=scales[:], in_=grouped[:])
+            return codes, scales
+
+        def gather_scales(name, window):
+            picked = new(name, J, U8)
+            nc.vector.tensor_copy(picked[:], window[:].indirect(slot_list[:]))
+            return picked
+
+        def product_half(name, half, word_win, col_scales, w_codes, w_scales):
+            cols = new(name + "_words", HALF, U32)
+            entries = slot_list[:, half * HALF // LIST_ROWS : (half + 1) * HALF // LIST_ROWS]
+            nc.vector.tensor_copy(cols[:], word_win[:].indirect(entries))
+            acc = ps.tile([P, HALF], F32, name=name)
+            nc.tensor.matmul_mx(
+                out=acc[:],
+                lhsT=w_codes[:].bitcast(FP8X4),
+                lhsT_scale=w_scales[:],
+                rhs=cols[:].bitcast(FP8X4),
+                rhs_scale=col_scales[:, half * HALF : (half + 1) * HALF],
+                start=True,
+                stop=True,
+            )
+            return acc
+
+        halves = [slice(h * HALF, (h + 1) * HALF) for h in range(2)]
+
+        w1_grouped = interleave("w1_grouped", w1_raw, nc.scalar.copy)
+        wo_grouped = interleave("wo_grouped", wo_raw, nc.scalar.copy)
+
+        tab_col_scales = gather_scales("tab_col_scales", tab_scale_win)
+        w1_codes, w1_scales = quantize("w1", w1_grouped)
+
+        neg_g = new("neg_g", 1)
+        nc.gpsimd.tensor_scalar(neg_g[:], g[:], -1.0, 0.0, ALU.mult, ALU.add)
+        no_gain = new("no_gain", 1)
+        nc.gpsimd.tensor_scalar(no_gain[:], g[:], neg_g[:], TINY, ALU.max, ALU.is_lt)
+        neg_g_safe = new("neg_g_safe", 1)
+        nc.gpsimd.tensor_tensor(neg_g_safe[:], neg_g[:], no_gain[:], ALU.subtract)
+        og2 = new("og2", 1)
+        nc.gpsimd.tensor_scalar(og2[:], o[:], 2.0, 0.0, ALU.mult, ALU.add)
+
+        pw_rows = ps.tile([P, M], F32, name="pw_rows")
+        for t in range(M // P):
+            nc.tensor.transpose(pw_rows[:, t * P : (t + 1) * P], pw_cols[:, t : t + 1].to_broadcast([P, P]), ident[:])
+        pw_sq = new("pw_sq", M)
+        nc.scalar.activation(out=pw_sq[:], in_=pw_rows[:], func=ACT.Square)
+
+        h1 = new("h1", J)
+        h2 = new("h2", J)
+        for h in range(2):
+            a = product_half("a%d" % h, h, tab_word_win, tab_col_scales, w1_codes, w1_scales)
+            nc.scalar.activation(out=h1[:, halves[h]], in_=a[:], func=ACT.Tanh, bias=b[:])
+        for h in range(2):
+            nc.scalar.activation(out=h2[:, halves[h]], in_=h1[:, halves[h]], func=ACT.Copy, scale=g[:])
+
+        dtab_col_scales = gather_scales("dtab_col_scales", dtab_scale_win)
+        wo_codes, wo_scales = quantize("wo", wo_grouped)
+        neg_inv_g = new("neg_inv_g", 1)
+        nc.vector.reciprocal(neg_inv_g[:], neg_g_safe[:])
+        dy_grouped = interleave("dy_grouped", dy_raw, nc.vector.tensor_copy)
+
+        u = new("u", M)
+        nc.vector.tensor_copy(u[:], h2[:].indirect(pick_list[:]))
+        dy_codes, dy_scales = quantize("dy", dy_grouped)
+        s = new("s", M)
+        nc.vector.tensor_tensor(s[:], u[:], pw_rows[:], ALU.mult)
+
+        c0 = ps.tile([P, M], F32, name="c0")
+        nc.tensor.matmul_mx(
+            out=c0[:],
+            lhsT=wo_codes[:].bitcast(FP8X4),
+            lhsT_scale=wo_scales[:],
+            rhs=dy_codes[:].bitcast(FP8X4),
+            rhs_scale=dy_scales[:],
+            start=True,
+            stop=True,
+        )
+
+        h1_sq = new("h1_sq", J)
+        nc.scalar.activation(out=h1_sq[:], in_=h1[:], func=ACT.Square)
+        slope = new("slope", J)
+        nc.scalar.activation(out=slope[:], in_=h1_sq[:], func=ACT.Identity, scale=neg_g[:], bias=g[:])
+        silu = new("silu", M)
+        nc.scalar.activation(out=silu[:], in_=s[:], func=ACT.Silu)
+        u_sq = new("u_sq", M)
+        nc.scalar.activation(out=u_sq[:], in_=u[:], func=ACT.Square)
+        pick_slope = new("pick_slope", M)
+        nc.scalar.activation(out=pick_slope[:], in_=u_sq[:], func=ACT.Identity, scale=neg_inv_g[:], bias=g[:])
+        th = new("th", M)
+        nc.scalar.activation(out=th[:], in_=s[:], func=ACT.Tanh, scale=0.5)
+        th_sq = new("th_sq", M)
+        nc.scalar.activation(out=th_sq[:], in_=th[:], func=ACT.Square, scale=0.5)
+        c_out = new("c_out", M)
+        nc.scalar.activation(out=c_out[:], in_=c0[:], func=ACT.Copy, scale=og2[:])
+
+        ta = [product_half("ta%d" % h, h, dtab_word_win, dtab_col_scales, w1_codes, w1_scales) for h in range(2)]
+        xh2 = new("xh2", J)
+        r = new("r", M, tag="ta0_words")
+        nc.vector.scalar_tensor_tensor(r[:], s[:], 0.5, silu[:], ALU.mult, ALU.subtract)
+        nc.vector.tensor_tensor(xh2[:, halves[0]], ta[0][:], slope[:, halves[0]], ALU.mult)
+        mm = new("mm", M)
+        nc.vector.scalar_tensor_tensor(mm[:], r[:], 2.0, pick_slope[:], ALU.add, ALU.mult)
+        nc.vector.tensor_tensor(xh2[:, halves[1]], ta[1][:], slope[:, halves[1]], ALU.mult)
+        qn = new("qn", M)
+        nc.vector.scalar_tensor_tensor(qn[:], th_sq[:], 0.25, pw_sq[:], ALU.subtract, ALU.mult)
+        vc = new("vc", M)
+        nc.vector.tensor_tensor(vc[:], xh2[:].indirect(pick_list[:]), c_out[:], ALU.mult)
+        nn = new("nn", M)
+        nc.vector.scalar_tensor_tensor(nn[:], mm[:], g[:], qn[:], ALU.subtract, ALU.mult)
+        gg = new("gg", M)
+        nc.vector.scalar_tensor_tensor(gg[:], silu[:], neg_inv_g[:], nn[:], ALU.mult, ALU.subtract)
+        nc.vector.tensor_tensor(placed[:].indirect(pick_list[:]), gg[:], vc[:], ALU.mult)
+
+        for h, queue in enumerate((nc.sync, nc.scalar)):
+            result = new("result%d" % h, HALF)
+            nc.vector.tensor_tensor(result[:], placed[:, halves[h]], base_sb[:, halves[h]], ALU.add)
+            queue.dma_start(out=out[:, halves[h]], in_=result[:])

@@ -1,7 +1,6 @@
 from contextlib import ExitStack
 
 import concourse.mybir as mybir
-from concourse.masks import make_identity
 
 K, R, F, T, J, M = 512, 128, 512, 2048, 512, 256
 FLOPS = 2 * K * R * J * 2 + 2 * F * R * M
@@ -29,16 +28,25 @@ def tile_attend_hvpickact_kernel(
     nc = tc.nc
     with ExitStack() as ctx:
         sb = ctx.enter_context(tc.tile_pool(name="sb", bufs=1))
+        shared = ctx.enter_context(tc.tile_pool(name="shared", bufs=1))
         ps = ctx.enter_context(tc.psum_pool(name="ps", bufs=1))
 
         def new(name, width, dtype=F32, tag=None):
             return sb.tile([P, width], dtype, name=name, tag=tag or name, align_bytes=64)
 
-        slot_list = sb.tile([P, J // LIST_ROWS], U16, name="slot_list")
-        nc.sync.dma_start(slot_list[:], offs)
+        def at(offset, name, shape, dtype=F32):
+            return shared.tile([P, *shape], dtype, name=name, align_bytes=64, offset=offset)
 
-        def load_scales(name, scales):
-            window = new(name, T, U8)
+        tab_at = 0
+        wo_at = tab_at + 4 * T
+        dy_at = wo_at + 4 * PACK * R
+        dtab_at = dy_at + 4 * PACK * M
+        base_at = dtab_at + 4 * T
+        ta_words_at = [base_at + 4 * J, base_at + 4 * J + 4 * HALF + M + R]
+        dy_scales_at = ta_words_at[0] + 4 * HALF
+        wo_scales_at = dy_scales_at + M
+
+        def load_scales(window, scales):
             nc.vector.memset(window[:].bitcast(I32), 0)
             for q in range(4):
                 nc.sync.dma_start(
@@ -46,173 +54,160 @@ def tile_attend_hvpickact_kernel(
                 )
             return window
 
-        def load_words(name, words):
-            window = new(name, T, U32)
+        def load_words(window, words):
             nc.sync.dma_start(out=window[:].bitcast(I32), in_=words[0].rearrange("p n t -> p (n t)").bitcast(I32))
             return window
 
-        def load_rows(name, rows):
-            raw = sb.tile([P, PACK, rows.shape[1]], F32, name=name)
+        def load_rows(raw, rows):
             nc.sync.dma_start(out=raw[:], in_=rows.rearrange("(p t) c -> p t c", t=PACK))
             return raw
 
-        def load_column(name, column):
-            tile = new(name, 1)
-            nc.gpsimd.dma_start(out=tile[:], in_=column)
-            return tile
-
-        w1_raw = load_rows("w1_raw", w1)
-        pick_list = sb.tile([P, M // LIST_ROWS], U16, name="pick_list")
-        nc.sync.dma_start(pick_list[:], offs2)
-        tab_scale_win = load_scales("tab_scale_win", tab_scales)
-        warm = new("warm", 1)
-        warm_out = new("warm_out", 1)
-        nc.gpsimd.memset(warm[:], 0.0)
-        nc.scalar.activation(out=warm_out[:], in_=warm[:], func=ACT.Silu)
-        tab_word_win = load_words("tab_word_win", tab_words)
-        dtab_scale_win = load_scales("dtab_scale_win", dtab_scales)
-        wo_raw = load_rows("wo_raw", wo)
-        dy_raw = load_rows("dy_raw", dy)
-        dtab_word_win = load_words("dtab_word_win", dtab_words)
-        base_sb = new("base_sb", J)
-        nc.sync.dma_start(out=base_sb[:], in_=base)
-
-        b = load_column("b", bias)
-        g = load_column("g", gain)
-        pw_cols = new("pw_cols", M // P)
-        with nc.allow_non_contiguous_dma(reason="one pick weight to a partition"):
-            nc.gpsimd.dma_start(out=pw_cols[:], in_=pw.rearrange("o (t p) -> p (o t)", p=P))
-        o = load_column("o", og)
-
-        placed = new("placed", J)
-        nc.vector.memset(placed[:], 0.0)
-        ident = new("ident", P)
-        make_identity(nc, ident[:])
-
-        def interleave(name, raw, copy):
-            width = raw.shape[2]
-            grouped = new(name, width * PACK, BF16)
+        def interleave(grouped, raw, copy):
             copy(
                 out=grouped[:].rearrange("p (c i t) -> p c t i", i=4, t=PACK),
                 in_=raw[:].rearrange("p t (c i) -> p c t i", i=4),
             )
             return grouped
 
-        def quantize(name, grouped):
-            width = grouped.shape[1] // PACK
-            codes = new(name + "_codes", width, U32)
-            scales = new(name + "_scales", width, U8)
+        def quantize(name, grouped, scales):
+            codes = new(name, grouped.shape[1] // PACK, U32)
             nc.vector.quantize_mx(out=codes[:].bitcast(FP8X4), scales=scales[:], in_=grouped[:])
             return codes, scales
 
-        def gather_scales(name, window):
-            picked = new(name, J, U8)
+        def gather_scales(picked, window):
             nc.vector.tensor_copy(picked[:], window[:].indirect(slot_list[:]))
             return picked
 
-        def product_half(name, half, word_win, col_scales, w_codes, w_scales):
-            cols = new(name + "_words", HALF, U32)
-            entries = slot_list[:, half * HALF // LIST_ROWS : (half + 1) * HALF // LIST_ROWS]
-            nc.vector.tensor_copy(cols[:], word_win[:].indirect(entries))
-            acc = ps.tile([P, HALF], F32, name=name)
+        def product(acc, stationary, moving_codes, moving_scales):
             nc.tensor.matmul_mx(
                 out=acc[:],
-                lhsT=w_codes[:].bitcast(FP8X4),
-                lhsT_scale=w_scales[:],
-                rhs=cols[:].bitcast(FP8X4),
-                rhs_scale=col_scales[:, half * HALF : (half + 1) * HALF],
+                lhsT=stationary[0][:].bitcast(FP8X4),
+                lhsT_scale=stationary[1][:],
+                rhs=moving_codes.bitcast(FP8X4),
+                rhs_scale=moving_scales,
                 start=True,
                 stop=True,
             )
             return acc
 
+        def product_half(name, half, cols, word_win, col_scales):
+            entries = slot_list[:, half * HALF // LIST_ROWS : (half + 1) * HALF // LIST_ROWS]
+            nc.vector.tensor_copy(cols[:], word_win[:].indirect(entries))
+            return product(ps.tile([P, HALF], F32, name=name), w1_mx, cols[:], col_scales[:, halves[half]])
+
         halves = [slice(h * HALF, (h + 1) * HALF) for h in range(2)]
 
-        w1_grouped = interleave("w1_grouped", w1_raw, nc.scalar.copy)
-        wo_grouped = interleave("wo_grouped", wo_raw, nc.scalar.copy)
+        slot_list = sb.tile([P, J // LIST_ROWS], U16, name="slot_list")
+        nc.sync.dma_start(slot_list[:], offs)
+        pick_list = sb.tile([P, M // LIST_ROWS], U16, name="pick_list")
+        nc.sync.dma_start(pick_list[:], offs2)
+        w1_raw = load_rows(sb.tile([P, PACK, R], F32, name="w1_raw", align_bytes=64), w1)
+        ones = at(tab_at, "ones", [P])
+        nc.vector.memset(ones[:], 1.0)
+        tab_scale_win = load_scales(new("tab_scale_win", T, U8), tab_scales)
+        column_number = new("column_number", P)
+        nc.vector.tensor_tensor_scan(column_number[:], ones[:], ones[:], 0.0, ALU.mult, ALU.add)
+        tab_word_win = load_words(at(tab_at, "tab_word_win", [T], U32), tab_words)
+        dtab_scale_win = load_scales(new("dtab_scale_win", T, U8), dtab_scales)
+        placed = new("placed", J)
+        nc.vector.memset(placed[:], 0.0)
+        warm_out = at(dy_at - 64, "warm_out", [32])
+        nc.scalar.activation(out=warm_out[:], in_=placed[:, 0:32], func=ACT.Silu)
+        wo_raw = load_rows(at(wo_at, "wo_raw", [PACK, R]), wo)
+        dy_raw = load_rows(at(dy_at, "dy_raw", [PACK, M]), dy)
 
-        tab_col_scales = gather_scales("tab_col_scales", tab_scale_win)
-        w1_codes, w1_scales = quantize("w1", w1_grouped)
+        columns = new("columns", 32)
+        b, g, pw_cols, o = columns[:, 0:1], columns[:, 8:9], columns[:, 16:18], columns[:, 24:25]
+        nc.gpsimd.dma_start(out=b, in_=bias)
+        nc.gpsimd.dma_start(out=g, in_=gain)
+        with nc.allow_non_contiguous_dma(reason="one pick weight to a partition"):
+            nc.gpsimd.dma_start(out=pw_cols, in_=pw.rearrange("o (t p) -> p (o t)", p=P))
+        row_number = new("row_number", 1)
+        nc.gpsimd.iota(row_number[:], pattern=[[1, 1]], base=1, channel_multiplier=1, allow_small_or_imprecise_dtypes=True)
+        nc.gpsimd.dma_start(out=o, in_=og)
 
-        neg_g = new("neg_g", 1)
-        nc.gpsimd.tensor_scalar(neg_g[:], g[:], -1.0, 0.0, ALU.mult, ALU.add)
-        no_gain = new("no_gain", 1)
-        nc.gpsimd.tensor_scalar(no_gain[:], g[:], neg_g[:], TINY, ALU.max, ALU.is_lt)
-        neg_g_safe = new("neg_g_safe", 1)
-        nc.gpsimd.tensor_tensor(neg_g_safe[:], neg_g[:], no_gain[:], ALU.subtract)
-        og2 = new("og2", 1)
-        nc.gpsimd.tensor_scalar(og2[:], o[:], 2.0, 0.0, ALU.mult, ALU.add)
-
-        pw_rows = ps.tile([P, M], F32, name="pw_rows")
-        for t in range(M // P):
-            nc.tensor.transpose(pw_rows[:, t * P : (t + 1) * P], pw_cols[:, t : t + 1].to_broadcast([P, P]), ident[:])
-        pw_sq = new("pw_sq", M)
-        nc.scalar.activation(out=pw_sq[:], in_=pw_rows[:], func=ACT.Square)
+        w1_grouped = interleave(at(base_at - PACK * R, "w1_grouped", [PACK * R], BF16), w1_raw, nc.scalar.copy)
+        tab_col_scales = gather_scales(new("tab_col_scales", J, U8), tab_scale_win)
+        w1_mx = quantize("w1_codes", w1_grouped, new("w1_scales", R, U8))
+        ident = new("ident", P, tag="tab_scale_win")
+        nc.vector.tensor_scalar(ident[:], column_number[:], row_number[:], None, ALU.is_equal)
+        dtab_word_win = load_words(at(dtab_at, "dtab_word_win", [T], U32), dtab_words)
+        base_sb = at(base_at, "base_sb", [J])
+        nc.sync.dma_start(out=base_sb[:], in_=base)
+        wo_grouped = interleave(new("wo_grouped", PACK * R, BF16), wo_raw, nc.scalar.copy)
 
         h1 = new("h1", J)
-        h2 = new("h2", J)
+        h2 = at(ta_words_at[0] + 64, "h2", [J])
         for h in range(2):
-            a = product_half("a%d" % h, h, tab_word_win, tab_col_scales, w1_codes, w1_scales)
-            nc.scalar.activation(out=h1[:, halves[h]], in_=a[:], func=ACT.Tanh, bias=b[:])
+            a = product_half("a%d" % h, h, new("a%d_words" % h, HALF, U32), tab_word_win, tab_col_scales)
+            nc.scalar.activation(out=h1[:, halves[h]], in_=a[:], func=ACT.Tanh, bias=b)
         for h in range(2):
-            nc.scalar.activation(out=h2[:, halves[h]], in_=h1[:, halves[h]], func=ACT.Copy, scale=g[:])
+            nc.scalar.activation(out=h2[:, halves[h]], in_=h1[:, halves[h]], func=ACT.Copy, scale=g)
 
-        dtab_col_scales = gather_scales("dtab_col_scales", dtab_scale_win)
-        wo_codes, wo_scales = quantize("wo", wo_grouped)
-        neg_inv_g = new("neg_inv_g", 1)
-        nc.vector.reciprocal(neg_inv_g[:], neg_g_safe[:])
-        dy_grouped = interleave("dy_grouped", dy_raw, nc.vector.tensor_copy)
+        neg_g = new("neg_g", 1)
+        nc.scalar.activation(out=neg_g[:], in_=g, func=ACT.Copy, scale=-1.0)
+        abs_g = new("abs_g", 1)
+        nc.scalar.activation(out=abs_g[:], in_=g, func=ACT.Abs)
+        safe_g = at(tab_at, "safe_g", [1])
+        nc.vector.scalar_tensor_tensor(safe_g[:], abs_g[:], TINY, g, ALU.is_lt, ALU.add)
+        dtab_col_scales = gather_scales(new("dtab_col_scales", J, U8, "a0_words"), dtab_scale_win)
+        inv_g = new("inv_g", 1)
+        nc.vector.reciprocal(inv_g[:], safe_g[:])
+        og2 = new("og2", 1)
+        nc.gpsimd.tensor_scalar(og2[:], o, -2.0, 0.0, ALU.mult, ALU.add)
+
+        pw_rows = ps.tile([P, M], F32, name="pw_rows", tag="a1")
+        for t in range(M // P):
+            nc.tensor.transpose(pw_rows[:, t * P : (t + 1) * P], pw_cols[:, t : t + 1].to_broadcast([P, P]), ident[:])
+
+        dy_grouped = interleave(new("dy_grouped", PACK * M, BF16, "dtab_scale_win"), dy_raw, nc.vector.tensor_copy)
 
         u = new("u", M)
         nc.vector.tensor_copy(u[:], h2[:].indirect(pick_list[:]))
-        dy_codes, dy_scales = quantize("dy", dy_grouped)
+        wo_mx = quantize("wo_codes", wo_grouped, at(wo_scales_at, "wo_scales", [R], U8))
         s = new("s", M)
         nc.vector.tensor_tensor(s[:], u[:], pw_rows[:], ALU.mult)
-
-        c0 = ps.tile([P, M], F32, name="c0")
-        nc.tensor.matmul_mx(
-            out=c0[:],
-            lhsT=wo_codes[:].bitcast(FP8X4),
-            lhsT_scale=wo_scales[:],
-            rhs=dy_codes[:].bitcast(FP8X4),
-            rhs_scale=dy_scales[:],
-            start=True,
-            stop=True,
-        )
+        dy_codes, dy_scales = quantize("dy_codes", dy_grouped, at(dy_scales_at, "dy_scales", [M], U8))
+        c0 = product(ps.tile([P, M], F32, name="c0"), wo_mx, dy_codes[:], dy_scales[:])
 
         h1_sq = new("h1_sq", J)
         nc.scalar.activation(out=h1_sq[:], in_=h1[:], func=ACT.Square)
         slope = new("slope", J)
-        nc.scalar.activation(out=slope[:], in_=h1_sq[:], func=ACT.Identity, scale=neg_g[:], bias=g[:])
+        nc.scalar.activation(out=slope[:], in_=h1_sq[:], func=ACT.Identity, scale=neg_g[:], bias=g)
         silu = new("silu", M)
         nc.scalar.activation(out=silu[:], in_=s[:], func=ACT.Silu)
         u_sq = new("u_sq", M)
         nc.scalar.activation(out=u_sq[:], in_=u[:], func=ACT.Square)
         pick_slope = new("pick_slope", M)
-        nc.scalar.activation(out=pick_slope[:], in_=u_sq[:], func=ACT.Identity, scale=neg_inv_g[:], bias=g[:])
+        nc.scalar.activation(out=pick_slope[:], in_=u_sq[:], func=ACT.Identity, scale=inv_g[:], bias=neg_g[:])
         th = new("th", M)
         nc.scalar.activation(out=th[:], in_=s[:], func=ACT.Tanh, scale=0.5)
         th_sq = new("th_sq", M)
         nc.scalar.activation(out=th_sq[:], in_=th[:], func=ACT.Square, scale=0.5)
+        pw_sq = new("pw_sq", M)
+        nc.scalar.activation(out=pw_sq[:], in_=pw_rows[:], func=ACT.Square)
         c_out = new("c_out", M)
         nc.scalar.activation(out=c_out[:], in_=c0[:], func=ACT.Copy, scale=og2[:])
 
-        ta = [product_half("ta%d" % h, h, dtab_word_win, dtab_col_scales, w1_codes, w1_scales) for h in range(2)]
+        ta = [
+            product_half("ta%d" % h, h, at(ta_words_at[h], "ta%d_words" % h, [HALF], U32), dtab_word_win, dtab_col_scales)
+            for h in range(2)
+        ]
         xh2 = new("xh2", J)
-        r = new("r", M, tag="ta0_words")
+        r = at(ta_words_at[0], "r", [M])
         nc.vector.scalar_tensor_tensor(r[:], s[:], 0.5, silu[:], ALU.mult, ALU.subtract)
         nc.vector.tensor_tensor(xh2[:, halves[0]], ta[0][:], slope[:, halves[0]], ALU.mult)
         mm = new("mm", M)
         nc.vector.scalar_tensor_tensor(mm[:], r[:], 2.0, pick_slope[:], ALU.add, ALU.mult)
-        nc.vector.tensor_tensor(xh2[:, halves[1]], ta[1][:], slope[:, halves[1]], ALU.mult)
-        qn = new("qn", M)
+        qn = at(ta_words_at[1], "qn", [M])
         nc.vector.scalar_tensor_tensor(qn[:], th_sq[:], 0.25, pw_sq[:], ALU.subtract, ALU.mult)
+        nc.vector.tensor_tensor(xh2[:, halves[1]], ta[1][:], slope[:, halves[1]], ALU.mult)
+        nn = new("nn", M)
+        nc.vector.scalar_tensor_tensor(nn[:], mm[:], g, qn[:], ALU.add, ALU.mult)
         vc = new("vc", M)
         nc.vector.tensor_tensor(vc[:], xh2[:].indirect(pick_list[:]), c_out[:], ALU.mult)
-        nn = new("nn", M)
-        nc.vector.scalar_tensor_tensor(nn[:], mm[:], g[:], qn[:], ALU.subtract, ALU.mult)
         gg = new("gg", M)
-        nc.vector.scalar_tensor_tensor(gg[:], silu[:], neg_inv_g[:], nn[:], ALU.mult, ALU.subtract)
+        nc.vector.scalar_tensor_tensor(gg[:], silu[:], inv_g[:], nn[:], ALU.mult, ALU.subtract)
         nc.vector.tensor_tensor(placed[:].indirect(pick_list[:]), gg[:], vc[:], ALU.mult)
 
         for h, queue in enumerate((nc.sync, nc.scalar)):

@@ -17,9 +17,22 @@ ACT = mybir.ActivationFunctionType
 
 P = 128
 PACK = 4
-HALF = J // 2
+QUADRANT = 32
+SCALE_ROWS = 4
 LIST_ROWS = 16
-TINY = 2.0**-126
+HALF = J // 2
+ALIGN = 64
+COLUMN_STEP = 8
+LINE = 4
+SMALLEST_NORMAL = 2.0**-126
+
+TAB_WORDS_AT = 0
+WO_RAW_AT = TAB_WORDS_AT + 4 * T
+DY_RAW_AT = WO_RAW_AT + 4 * PACK * R
+DTAB_WORDS_AT = DY_RAW_AT + 4 * PACK * M
+WO_SCALES_AT = DTAB_WORDS_AT + 4 * T
+DY_GROUPED_AT = WO_SCALES_AT + R
+H2_AT = DY_GROUPED_AT + 2 * PACK * M
 
 
 def tile_attend_hvpickact_kernel(
@@ -32,25 +45,17 @@ def tile_attend_hvpickact_kernel(
         ps = ctx.enter_context(tc.psum_pool(name="ps", bufs=1))
 
         def new(name, width, dtype=F32, tag=None):
-            return sb.tile([P, width], dtype, name=name, tag=tag or name, align_bytes=64)
+            return sb.tile([P, width], dtype, name=name, tag=tag or name, align_bytes=ALIGN)
 
         def at(offset, name, shape, dtype=F32):
-            return shared.tile([P, *shape], dtype, name=name, align_bytes=64, offset=offset)
-
-        tab_at = 0
-        wo_at = tab_at + 4 * T
-        dy_at = wo_at + 4 * PACK * R
-        dtab_at = dy_at + 4 * PACK * M
-        base_at = dtab_at + 4 * T
-        ta_words_at = [base_at + 4 * J, base_at + 4 * J + 4 * HALF + M + R]
-        dy_scales_at = ta_words_at[0] + 4 * HALF
-        wo_scales_at = dy_scales_at + M
+            return shared.tile([P, *shape], dtype, name=name, align_bytes=ALIGN, offset=offset)
 
         def load_scales(window, scales):
             nc.vector.memset(window[:].bitcast(I32), 0)
-            for q in range(4):
+            for q in range(P // QUADRANT):
                 nc.sync.dma_start(
-                    out=window[32 * q : 32 * q + 4, :].bitcast(I32), in_=scales[0, 4 * q : 4 * q + 4, :].bitcast(I32)
+                    out=window[QUADRANT * q : QUADRANT * q + SCALE_ROWS, :].bitcast(I32),
+                    in_=scales[0, SCALE_ROWS * q : SCALE_ROWS * (q + 1), :].bitcast(I32),
                 )
             return window
 
@@ -64,8 +69,8 @@ def tile_attend_hvpickact_kernel(
 
         def interleave(grouped, raw, copy):
             copy(
-                out=grouped[:].rearrange("p (c i t) -> p c t i", i=4, t=PACK),
-                in_=raw[:].rearrange("p t (c i) -> p c t i", i=4),
+                out=grouped[:].rearrange("p (c i t) -> p c t i", i=LINE, t=PACK),
+                in_=raw[:].rearrange("p t (c i) -> p c t i", i=LINE),
             )
             return grouped
 
@@ -74,9 +79,9 @@ def tile_attend_hvpickact_kernel(
             nc.vector.quantize_mx(out=codes[:].bitcast(FP8X4), scales=scales[:], in_=grouped[:])
             return codes, scales
 
-        def gather_scales(picked, window):
-            nc.vector.tensor_copy(picked[:], window[:].indirect(slot_list[:]))
-            return picked
+        def gather_scales(listed, window):
+            nc.vector.tensor_copy(listed[:], window[:].indirect(slot_list[:]))
+            return listed
 
         def product(acc, stationary, moving_codes, moving_scales):
             nc.tensor.matmul_mx(
@@ -90,10 +95,10 @@ def tile_attend_hvpickact_kernel(
             )
             return acc
 
-        def product_half(name, half, cols, word_win, col_scales):
+        def product_half(name, half, listed_words, word_window, listed_scales):
             entries = slot_list[:, half * HALF // LIST_ROWS : (half + 1) * HALF // LIST_ROWS]
-            nc.vector.tensor_copy(cols[:], word_win[:].indirect(entries))
-            return product(ps.tile([P, HALF], F32, name=name), w1_mx, cols[:], col_scales[:, halves[half]])
+            nc.vector.tensor_copy(listed_words[:], word_window[:].indirect(entries))
+            return product(ps.tile([P, HALF], F32, name=name), w1_mx, listed_words[:], listed_scales[:, halves[half]])
 
         halves = [slice(h * HALF, (h + 1) * HALF) for h in range(2)]
 
@@ -101,73 +106,80 @@ def tile_attend_hvpickact_kernel(
         nc.sync.dma_start(slot_list[:], offs)
         pick_list = sb.tile([P, M // LIST_ROWS], U16, name="pick_list")
         nc.sync.dma_start(pick_list[:], offs2)
-        w1_raw = load_rows(sb.tile([P, PACK, R], F32, name="w1_raw", align_bytes=64), w1)
-        ones = at(tab_at, "ones", [P])
+        w1_raw = load_rows(at(DY_RAW_AT, "w1_raw", [PACK, R]), w1)
+
+        ones = at(TAB_WORDS_AT, "ones", [P])
         nc.vector.memset(ones[:], 1.0)
-        tab_scale_win = load_scales(new("tab_scale_win", T, U8), tab_scales)
+        tab_scale_window = load_scales(new("tab_scale_window", T, U8), tab_scales)
         column_number = new("column_number", P)
         nc.vector.tensor_tensor_scan(column_number[:], ones[:], ones[:], 0.0, ALU.mult, ALU.add)
-        tab_word_win = load_words(at(tab_at, "tab_word_win", [T], U32), tab_words)
-        dtab_scale_win = load_scales(new("dtab_scale_win", T, U8), dtab_scales)
+        tab_word_window = load_words(at(TAB_WORDS_AT, "tab_word_window", [T], U32), tab_words)
+        dtab_scale_window = load_scales(at(DY_GROUPED_AT - ALIGN, "dtab_scale_window", [T], U8), dtab_scales)
         placed = new("placed", J)
         nc.vector.memset(placed[:], 0.0)
-        warm_out = at(dy_at - 64, "warm_out", [32])
-        nc.scalar.activation(out=warm_out[:], in_=placed[:, 0:32], func=ACT.Silu)
-        wo_raw = load_rows(at(wo_at, "wo_raw", [PACK, R]), wo)
-        dy_raw = load_rows(at(dy_at, "dy_raw", [PACK, M]), dy)
 
-        columns = new("columns", 32)
-        b, g, pw_cols, o = columns[:, 0:1], columns[:, 8:9], columns[:, 16:18], columns[:, 24:25]
-        nc.gpsimd.dma_start(out=b, in_=bias)
+        zero = at(WO_RAW_AT, "zero", [1])
+        nc.vector.memset(zero[:], 0.0)
+        zero_bias = new("zero_bias", 1)
+        nc.scalar.activation(out=zero_bias[:], in_=zero[:], func=ACT.Silu)
+        wo_raw = load_rows(at(WO_RAW_AT, "wo_raw", [PACK, R]), wo)
+
+        row_number = new("row_number", 1)
+        nc.gpsimd.iota(row_number[:], pattern=[[1, 1]], base=1, channel_multiplier=1, allow_small_or_imprecise_dtypes=True)
+        identity = new("identity", P)
+        nc.vector.tensor_scalar(identity[:], column_number[:], row_number[:], None, ALU.is_equal)
+
+        columns = new("columns", 4 * COLUMN_STEP)
+        bias_col, g, pw_cols, og_col = [
+            columns[:, i * COLUMN_STEP : i * COLUMN_STEP + width] for i, width in enumerate((1, 1, M // P, 1))
+        ]
+        nc.gpsimd.dma_start(out=bias_col, in_=bias)
         nc.gpsimd.dma_start(out=g, in_=gain)
         with nc.allow_non_contiguous_dma(reason="one pick weight to a partition"):
             nc.gpsimd.dma_start(out=pw_cols, in_=pw.rearrange("o (t p) -> p (o t)", p=P))
-        row_number = new("row_number", 1)
-        nc.gpsimd.iota(row_number[:], pattern=[[1, 1]], base=1, channel_multiplier=1, allow_small_or_imprecise_dtypes=True)
-        nc.gpsimd.dma_start(out=o, in_=og)
+        nc.gpsimd.dma_start(out=og_col, in_=og)
 
-        w1_grouped = interleave(at(base_at - PACK * R, "w1_grouped", [PACK * R], BF16), w1_raw, nc.scalar.copy)
-        tab_col_scales = gather_scales(new("tab_col_scales", J, U8), tab_scale_win)
+        w1_grouped = interleave(at(DTAB_WORDS_AT, "w1_grouped", [PACK * R], BF16), w1_raw, nc.scalar.copy)
+        dy_raw = load_rows(at(DY_RAW_AT, "dy_raw", [PACK, M]), dy)
+        tab_listed_scales = gather_scales(new("tab_listed_scales", J, U8), tab_scale_window)
         w1_mx = quantize("w1_codes", w1_grouped, new("w1_scales", R, U8))
-        ident = new("ident", P, tag="tab_scale_win")
-        nc.vector.tensor_scalar(ident[:], column_number[:], row_number[:], None, ALU.is_equal)
-        dtab_word_win = load_words(at(dtab_at, "dtab_word_win", [T], U32), dtab_words)
-        base_sb = at(base_at, "base_sb", [J])
-        nc.sync.dma_start(out=base_sb[:], in_=base)
+        dtab_word_window = load_words(at(DTAB_WORDS_AT, "dtab_word_window", [T], U32), dtab_words)
         wo_grouped = interleave(new("wo_grouped", PACK * R, BF16), wo_raw, nc.scalar.copy)
 
-        h1 = new("h1", J)
-        h2 = at(ta_words_at[0] + 64, "h2", [J])
+        h1 = at(WO_RAW_AT, "h1", [J])
+        h2 = at(H2_AT, "h2", [J])
         for h in range(2):
-            a = product_half("a%d" % h, h, new("a%d_words" % h, HALF, U32), tab_word_win, tab_col_scales)
-            nc.scalar.activation(out=h1[:, halves[h]], in_=a[:], func=ACT.Tanh, bias=b)
+            a = product_half("a%d" % h, h, new("a%d_words" % h, HALF, U32), tab_word_window, tab_listed_scales)
+            nc.scalar.activation(out=h1[:, halves[h]], in_=a[:], func=ACT.Tanh, bias=bias_col)
         for h in range(2):
             nc.scalar.activation(out=h2[:, halves[h]], in_=h1[:, halves[h]], func=ACT.Copy, scale=g)
 
+        base_sb = at(TAB_WORDS_AT + ALIGN, "base_sb", [J])
+        nc.sync.dma_start(out=base_sb[:], in_=base)
         neg_g = new("neg_g", 1)
         nc.scalar.activation(out=neg_g[:], in_=g, func=ACT.Copy, scale=-1.0)
         abs_g = new("abs_g", 1)
         nc.scalar.activation(out=abs_g[:], in_=g, func=ACT.Abs)
-        safe_g = at(tab_at, "safe_g", [1])
-        nc.vector.scalar_tensor_tensor(safe_g[:], abs_g[:], TINY, g, ALU.is_lt, ALU.add)
-        dtab_col_scales = gather_scales(new("dtab_col_scales", J, U8, "a0_words"), dtab_scale_win)
+        safe_g = at(TAB_WORDS_AT, "safe_g", [1])
+        nc.vector.scalar_tensor_tensor(safe_g[:], abs_g[:], SMALLEST_NORMAL, g, ALU.is_lt, ALU.add)
+
+        dtab_listed_scales = gather_scales(new("dtab_listed_scales", J, U8, "a0_words"), dtab_scale_window)
         inv_g = new("inv_g", 1)
         nc.vector.reciprocal(inv_g[:], safe_g[:])
-        og2 = new("og2", 1)
-        nc.gpsimd.tensor_scalar(og2[:], o, -2.0, 0.0, ALU.mult, ALU.add)
+        neg_two_og = new("neg_two_og", 1)
+        nc.gpsimd.tensor_scalar(neg_two_og[:], og_col, -2.0, 0.0, ALU.mult, ALU.add)
+        wo_mx = quantize("wo_codes", wo_grouped, at(WO_SCALES_AT, "wo_scales", [R], U8))
+        dy_grouped = interleave(at(DY_GROUPED_AT, "dy_grouped", [PACK * M], BF16), dy_raw, nc.vector.tensor_copy)
 
         pw_rows = ps.tile([P, M], F32, name="pw_rows", tag="a1")
         for t in range(M // P):
-            nc.tensor.transpose(pw_rows[:, t * P : (t + 1) * P], pw_cols[:, t : t + 1].to_broadcast([P, P]), ident[:])
+            nc.tensor.transpose(pw_rows[:, t * P : (t + 1) * P], pw_cols[:, t : t + 1].to_broadcast([P, P]), identity[:])
 
-        dy_grouped = interleave(new("dy_grouped", PACK * M, BF16, "dtab_scale_win"), dy_raw, nc.vector.tensor_copy)
-
-        u = new("u", M)
+        u = at(DY_RAW_AT, "u", [M])
         nc.vector.tensor_copy(u[:], h2[:].indirect(pick_list[:]))
-        wo_mx = quantize("wo_codes", wo_grouped, at(wo_scales_at, "wo_scales", [R], U8))
+        dy_codes, dy_scales = quantize("dy_codes", dy_grouped, new("dy_scales", M, U8))
         s = new("s", M)
         nc.vector.tensor_tensor(s[:], u[:], pw_rows[:], ALU.mult)
-        dy_codes, dy_scales = quantize("dy_codes", dy_grouped, at(dy_scales_at, "dy_scales", [M], U8))
         c0 = product(ps.tile([P, M], F32, name="c0"), wo_mx, dy_codes[:], dy_scales[:])
 
         h1_sq = new("h1_sq", J)
@@ -175,40 +187,43 @@ def tile_attend_hvpickact_kernel(
         slope = new("slope", J)
         nc.scalar.activation(out=slope[:], in_=h1_sq[:], func=ACT.Identity, scale=neg_g[:], bias=g)
         silu = new("silu", M)
-        nc.scalar.activation(out=silu[:], in_=s[:], func=ACT.Silu)
+        nc.scalar.activation(out=silu[:], in_=s[:], func=ACT.Silu, bias=zero_bias[:])
         u_sq = new("u_sq", M)
         nc.scalar.activation(out=u_sq[:], in_=u[:], func=ACT.Square)
-        pick_slope = new("pick_slope", M)
-        nc.scalar.activation(out=pick_slope[:], in_=u_sq[:], func=ACT.Identity, scale=inv_g[:], bias=neg_g[:])
-        th = new("th", M)
-        nc.scalar.activation(out=th[:], in_=s[:], func=ACT.Tanh, scale=0.5)
-        th_sq = new("th_sq", M)
-        nc.scalar.activation(out=th_sq[:], in_=th[:], func=ACT.Square, scale=0.5)
+        neg_pick_slope = new("neg_pick_slope", M)
+        nc.scalar.activation(out=neg_pick_slope[:], in_=u_sq[:], func=ACT.Identity, scale=inv_g[:], bias=neg_g[:])
+        tanh_half = new("tanh_half", M)
+        nc.scalar.activation(out=tanh_half[:], in_=s[:], func=ACT.Tanh, scale=0.5)
+        quarter_tanh_sq = new("quarter_tanh_sq", M)
+        nc.scalar.activation(out=quarter_tanh_sq[:], in_=tanh_half[:], func=ACT.Square, scale=0.5)
         pw_sq = new("pw_sq", M)
         nc.scalar.activation(out=pw_sq[:], in_=pw_rows[:], func=ACT.Square)
-        c_out = new("c_out", M)
-        nc.scalar.activation(out=c_out[:], in_=c0[:], func=ACT.Copy, scale=og2[:])
+        c0_out = new("c0_out", M)
+        nc.scalar.activation(out=c0_out[:], in_=c0[:], func=ACT.Copy, scale=neg_two_og[:])
 
         ta = [
-            product_half("ta%d" % h, h, at(ta_words_at[h], "ta%d_words" % h, [HALF], U32), dtab_word_win, dtab_col_scales)
+            product_half(
+                "ta%d" % h, h, at(H2_AT + 4 * HALF * h, "ta%d_words" % h, [HALF], U32), dtab_word_window, dtab_listed_scales
+            )
             for h in range(2)
         ]
+
+        neg_half_st = at(DTAB_WORDS_AT, "neg_half_st", [M])
+        nc.vector.scalar_tensor_tensor(neg_half_st[:], s[:], 0.5, silu[:], ALU.mult, ALU.subtract)
+        neg_weight = at(DTAB_WORDS_AT + 4 * M, "neg_weight", [M])
+        nc.vector.scalar_tensor_tensor(neg_weight[:], quarter_tanh_sq[:], 0.25, pw_sq[:], ALU.subtract, ALU.mult)
+        neg_curved = new("neg_curved", M)
+        nc.vector.scalar_tensor_tensor(neg_curved[:], neg_half_st[:], 2.0, neg_pick_slope[:], ALU.add, ALU.mult)
         xh2 = new("xh2", J)
-        r = at(ta_words_at[0], "r", [M])
-        nc.vector.scalar_tensor_tensor(r[:], s[:], 0.5, silu[:], ALU.mult, ALU.subtract)
         nc.vector.tensor_tensor(xh2[:, halves[0]], ta[0][:], slope[:, halves[0]], ALU.mult)
-        mm = new("mm", M)
-        nc.vector.scalar_tensor_tensor(mm[:], r[:], 2.0, pick_slope[:], ALU.add, ALU.mult)
-        qn = at(ta_words_at[1], "qn", [M])
-        nc.vector.scalar_tensor_tensor(qn[:], th_sq[:], 0.25, pw_sq[:], ALU.subtract, ALU.mult)
+        weighted = new("weighted", M)
+        nc.vector.scalar_tensor_tensor(weighted[:], neg_curved[:], g, neg_weight[:], ALU.add, ALU.mult)
         nc.vector.tensor_tensor(xh2[:, halves[1]], ta[1][:], slope[:, halves[1]], ALU.mult)
-        nn = new("nn", M)
-        nc.vector.scalar_tensor_tensor(nn[:], mm[:], g, qn[:], ALU.add, ALU.mult)
-        vc = new("vc", M)
-        nc.vector.tensor_tensor(vc[:], xh2[:].indirect(pick_list[:]), c_out[:], ALU.mult)
-        gg = new("gg", M)
-        nc.vector.scalar_tensor_tensor(gg[:], silu[:], inv_g[:], nn[:], ALU.mult, ALU.subtract)
-        nc.vector.tensor_tensor(placed[:].indirect(pick_list[:]), gg[:], vc[:], ALU.mult)
+        neg_bracket = new("neg_bracket", M)
+        nc.vector.scalar_tensor_tensor(neg_bracket[:], silu[:], inv_g[:], weighted[:], ALU.mult, ALU.subtract)
+        v_c0 = new("v_c0", M)
+        nc.vector.tensor_tensor(v_c0[:], xh2[:].indirect(pick_list[:]), c0_out[:], ALU.mult)
+        nc.vector.tensor_tensor(placed[:].indirect(pick_list[:]), neg_bracket[:], v_c0[:], ALU.mult)
 
         for h, queue in enumerate((nc.sync, nc.scalar)):
             result = new("result%d" % h, HALF)

from contextlib import ExitStack

import concourse.mybir as mybir

K, R, F, T, J, M = 512, 128, 512, 2048, 512, 256
FLOPS = 2 * K * R * J * 2 + 2 * F * R * M

F32 = mybir.dt.float32
BF16 = mybir.dt.bfloat16
I32 = mybir.dt.int32
U32 = mybir.dt.uint32
U16 = mybir.dt.uint16
U8 = mybir.dt.uint8
FP8X4 = mybir.dt.float8_e4m3fn_x4
ALU = mybir.AluOpType
ACT = mybir.ActivationFunctionType

P = 128
PACK = 4
QUADRANT = 32
SCALE_ROWS = 4
LIST_ROWS = 16
HALF = J // 2
ALIGN = 64
COLUMN_STEP = 8
LINE = 4
SMALLEST_NORMAL = 2.0**-126

TAB_WORDS_AT = 0
WO_RAW_AT = TAB_WORDS_AT + 4 * T
DY_RAW_AT = WO_RAW_AT + 4 * PACK * R
DTAB_WORDS_AT = DY_RAW_AT + 4 * PACK * M
WO_SCALES_AT = DTAB_WORDS_AT + 4 * T
DY_GROUPED_AT = WO_SCALES_AT + R
H2_AT = DY_GROUPED_AT + 2 * PACK * M


def tile_attend_hvpickact_kernel(
    tc, tab_words, tab_scales, w1, bias, gain, pw, wo, dy, dtab_words, dtab_scales, og, base, offs, offs2, out
):
    nc = tc.nc
    with ExitStack() as ctx:
        sb = ctx.enter_context(tc.tile_pool(name="sb", bufs=1))
        shared = ctx.enter_context(tc.tile_pool(name="shared", bufs=1))
        ps = ctx.enter_context(tc.psum_pool(name="ps", bufs=1))

        def new(name, width, dtype=F32, tag=None):
            return sb.tile([P, width], dtype, name=name, tag=tag or name, align_bytes=ALIGN)

        def at(offset, name, shape, dtype=F32):
            return shared.tile([P, *shape], dtype, name=name, align_bytes=ALIGN, offset=offset)

        def load_scales(window, scales):
            nc.vector.memset(window[:].bitcast(I32), 0)
            for q in range(P // QUADRANT):
                nc.sync.dma_start(
                    out=window[QUADRANT * q : QUADRANT * q + SCALE_ROWS, :].bitcast(I32),
                    in_=scales[0, SCALE_ROWS * q : SCALE_ROWS * (q + 1), :].bitcast(I32),
                )
            return window

        def load_words(window, words):
            nc.sync.dma_start(out=window[:].bitcast(I32), in_=words[0].rearrange("p n t -> p (n t)").bitcast(I32))
            return window

        def load_rows(raw, rows):
            nc.sync.dma_start(out=raw[:], in_=rows.rearrange("(p t) c -> p t c", t=PACK))
            return raw

        def interleave(grouped, raw, copy):
            copy(
                out=grouped[:].rearrange("p (c i t) -> p c t i", i=LINE, t=PACK),
                in_=raw[:].rearrange("p t (c i) -> p c t i", i=LINE),
            )
            return grouped

        def quantize(name, grouped, scales):
            codes = new(name, grouped.shape[1] // PACK, U32)
            nc.vector.quantize_mx(out=codes[:].bitcast(FP8X4), scales=scales[:], in_=grouped[:])
            return codes, scales

        def gather_scales(listed, window):
            nc.vector.tensor_copy(listed[:], window[:].indirect(slot_list[:]))
            return listed

        def product(acc, stationary, moving_codes, moving_scales):
            nc.tensor.matmul_mx(
                out=acc[:],
                lhsT=stationary[0][:].bitcast(FP8X4),
                lhsT_scale=stationary[1][:],
                rhs=moving_codes.bitcast(FP8X4),
                rhs_scale=moving_scales,
                start=True,
                stop=True,
            )
            return acc

        def product_half(name, half, listed_words, word_window, listed_scales):
            entries = slot_list[:, half * HALF // LIST_ROWS : (half + 1) * HALF // LIST_ROWS]
            nc.vector.tensor_copy(listed_words[:], word_window[:].indirect(entries))
            return product(ps.tile([P, HALF], F32, name=name), w1_mx, listed_words[:], listed_scales[:, halves[half]])

        halves = [slice(h * HALF, (h + 1) * HALF) for h in range(2)]

        slot_list = sb.tile([P, J // LIST_ROWS], U16, name="slot_list")
        nc.sync.dma_start(slot_list[:], offs)
        pick_list = sb.tile([P, M // LIST_ROWS], U16, name="pick_list")
        nc.sync.dma_start(pick_list[:], offs2)
        w1_raw = load_rows(at(DY_RAW_AT, "w1_raw", [PACK, R]), w1)

        ones = at(TAB_WORDS_AT, "ones", [P])
        nc.vector.memset(ones[:], 1.0)
        tab_scale_window = load_scales(new("tab_scale_window", T, U8), tab_scales)
        column_number = new("column_number", P)
        nc.vector.tensor_tensor_scan(column_number[:], ones[:], ones[:], 0.0, ALU.mult, ALU.add)
        tab_word_window = load_words(at(TAB_WORDS_AT, "tab_word_window", [T], U32), tab_words)
        dtab_scale_window = load_scales(at(DY_GROUPED_AT - ALIGN, "dtab_scale_window", [T], U8), dtab_scales)
        placed = new("placed", J)
        nc.vector.memset(placed[:], 0.0)

        zero = at(WO_RAW_AT, "zero", [1])
        nc.vector.memset(zero[:], 0.0)
        zero_bias = new("zero_bias", 1)
        nc.scalar.activation(out=zero_bias[:], in_=zero[:], func=ACT.Silu)
        wo_raw = load_rows(at(WO_RAW_AT, "wo_raw", [PACK, R]), wo)

        row_number = new("row_number", 1)
        nc.gpsimd.iota(row_number[:], pattern=[[1, 1]], base=1, channel_multiplier=1, allow_small_or_imprecise_dtypes=True)
        identity = new("identity", P)
        nc.vector.tensor_scalar(identity[:], column_number[:], row_number[:], None, ALU.is_equal)

        columns = new("columns", 4 * COLUMN_STEP)
        bias_col, g, pw_cols, og_col = [
            columns[:, i * COLUMN_STEP : i * COLUMN_STEP + width] for i, width in enumerate((1, 1, M // P, 1))
        ]
        nc.gpsimd.dma_start(out=bias_col, in_=bias)
        nc.gpsimd.dma_start(out=g, in_=gain)
        with nc.allow_non_contiguous_dma(reason="one pick weight to a partition"):
            nc.gpsimd.dma_start(out=pw_cols, in_=pw.rearrange("o (t p) -> p (o t)", p=P))
        nc.gpsimd.dma_start(out=og_col, in_=og)

        w1_grouped = interleave(at(DTAB_WORDS_AT, "w1_grouped", [PACK * R], BF16), w1_raw, nc.scalar.copy)
        dy_raw = load_rows(at(DY_RAW_AT, "dy_raw", [PACK, M]), dy)
        tab_listed_scales = gather_scales(new("tab_listed_scales", J, U8), tab_scale_window)
        w1_mx = quantize("w1_codes", w1_grouped, new("w1_scales", R, U8))
        dtab_word_window = load_words(at(DTAB_WORDS_AT, "dtab_word_window", [T], U32), dtab_words)
        wo_grouped = interleave(new("wo_grouped", PACK * R, BF16), wo_raw, nc.scalar.copy)

        h1 = at(WO_RAW_AT, "h1", [J])
        h2 = at(H2_AT, "h2", [J])
        for h in range(2):
            a = product_half("a%d" % h, h, new("a%d_words" % h, HALF, U32), tab_word_window, tab_listed_scales)
            nc.scalar.activation(out=h1[:, halves[h]], in_=a[:], func=ACT.Tanh, bias=bias_col)
        for h in range(2):
            nc.scalar.activation(out=h2[:, halves[h]], in_=h1[:, halves[h]], func=ACT.Copy, scale=g)

        base_sb = at(TAB_WORDS_AT + ALIGN, "base_sb", [J])
        nc.sync.dma_start(out=base_sb[:], in_=base)
        neg_g = new("neg_g", 1)
        nc.scalar.activation(out=neg_g[:], in_=g, func=ACT.Copy, scale=-1.0)
        abs_g = new("abs_g", 1)
        nc.scalar.activation(out=abs_g[:], in_=g, func=ACT.Abs)
        safe_g = at(TAB_WORDS_AT, "safe_g", [1])
        nc.vector.scalar_tensor_tensor(safe_g[:], abs_g[:], SMALLEST_NORMAL, g, ALU.is_lt, ALU.add)

        dtab_listed_scales = gather_scales(new("dtab_listed_scales", J, U8, "a0_words"), dtab_scale_window)
        inv_g = new("inv_g", 1)
        nc.vector.reciprocal(inv_g[:], safe_g[:])
        neg_two_og = new("neg_two_og", 1)
        nc.gpsimd.tensor_scalar(neg_two_og[:], og_col, -2.0, 0.0, ALU.mult, ALU.add)
        wo_mx = quantize("wo_codes", wo_grouped, at(WO_SCALES_AT, "wo_scales", [R], U8))
        dy_grouped = interleave(at(DY_GROUPED_AT, "dy_grouped", [PACK * M], BF16), dy_raw, nc.vector.tensor_copy)

        pw_rows = ps.tile([P, M], F32, name="pw_rows", tag="a1")
        for t in range(M // P):
            nc.tensor.transpose(pw_rows[:, t * P : (t + 1) * P], pw_cols[:, t : t + 1].to_broadcast([P, P]), identity[:])

        u = at(DY_RAW_AT, "u", [M])
        nc.vector.tensor_copy(u[:], h2[:].indirect(pick_list[:]))
        dy_codes, dy_scales = quantize("dy_codes", dy_grouped, new("dy_scales", M, U8))
        s = new("s", M)
        nc.vector.tensor_tensor(s[:], u[:], pw_rows[:], ALU.mult)
        c0 = product(ps.tile([P, M], F32, name="c0"), wo_mx, dy_codes[:], dy_scales[:])

        h1_sq = new("h1_sq", J)
        nc.scalar.activation(out=h1_sq[:], in_=h1[:], func=ACT.Square)
        slope = new("slope", J)
        nc.scalar.activation(out=slope[:], in_=h1_sq[:], func=ACT.Identity, scale=neg_g[:], bias=g)
        silu = new("silu", M)
        nc.scalar.activation(out=silu[:], in_=s[:], func=ACT.Silu, bias=zero_bias[:])
        u_sq = new("u_sq", M)
        nc.scalar.activation(out=u_sq[:], in_=u[:], func=ACT.Square)
        neg_pick_slope = new("neg_pick_slope", M)
        nc.scalar.activation(out=neg_pick_slope[:], in_=u_sq[:], func=ACT.Identity, scale=inv_g[:], bias=neg_g[:])
        tanh_half = new("tanh_half", M)
        nc.scalar.activation(out=tanh_half[:], in_=s[:], func=ACT.Tanh, scale=0.5)
        quarter_tanh_sq = new("quarter_tanh_sq", M)
        nc.scalar.activation(out=quarter_tanh_sq[:], in_=tanh_half[:], func=ACT.Square, scale=0.5)
        pw_sq = new("pw_sq", M)
        nc.scalar.activation(out=pw_sq[:], in_=pw_rows[:], func=ACT.Square)
        c0_out = new("c0_out", M)
        nc.scalar.activation(out=c0_out[:], in_=c0[:], func=ACT.Copy, scale=neg_two_og[:])

        ta = [
            product_half(
                "ta%d" % h, h, at(H2_AT + 4 * HALF * h, "ta%d_words" % h, [HALF], U32), dtab_word_window, dtab_listed_scales
            )
            for h in range(2)
        ]

        neg_half_st = at(DTAB_WORDS_AT, "neg_half_st", [M])
        nc.vector.scalar_tensor_tensor(neg_half_st[:], s[:], 0.5, silu[:], ALU.mult, ALU.subtract)
        neg_weight = at(DTAB_WORDS_AT + 4 * M, "neg_weight", [M])
        nc.vector.scalar_tensor_tensor(neg_weight[:], quarter_tanh_sq[:], 0.25, pw_sq[:], ALU.subtract, ALU.mult)
        neg_curved = new("neg_curved", M)
        nc.vector.scalar_tensor_tensor(neg_curved[:], neg_half_st[:], 2.0, neg_pick_slope[:], ALU.add, ALU.mult)
        xh2 = new("xh2", J)
        nc.vector.tensor_tensor(xh2[:, halves[0]], ta[0][:], slope[:, halves[0]], ALU.mult)
        weighted = new("weighted", M)
        nc.vector.scalar_tensor_tensor(weighted[:], neg_curved[:], g, neg_weight[:], ALU.add, ALU.mult)
        nc.vector.tensor_tensor(xh2[:, halves[1]], ta[1][:], slope[:, halves[1]], ALU.mult)
        neg_bracket = new("neg_bracket", M)
        nc.vector.scalar_tensor_tensor(neg_bracket[:], silu[:], inv_g[:], weighted[:], ALU.mult, ALU.subtract)
        v_c0 = new("v_c0", M)
        nc.vector.tensor_tensor(v_c0[:], xh2[:].indirect(pick_list[:]), c0_out[:], ALU.mult)
        nc.vector.tensor_tensor(placed[:].indirect(pick_list[:]), neg_bracket[:], v_c0[:], ALU.mult)

        for h, queue in enumerate((nc.sync, nc.scalar)):
            result = new("result%d" % h, HALF)
            nc.vector.tensor_tensor(result[:], placed[:, halves[h]], base_sb[:, halves[h]], ALU.add)
            queue.dma_start(out=out[:, halves[h]], in_=result[:])
